import numpy as np
import ml_dtypes


def mxq(x, axis, fmt="e4m3"):
    dtype, down = {"e4m3": (ml_dtypes.float8_e4m3fn, 7), "e5m2": (ml_dtypes.float8_e5m2, 14)}[fmt]
    v = np.moveaxis(np.asarray(x, np.float32).astype(ml_dtypes.bfloat16).astype(np.float64), axis, -1)
    blocks = v.reshape(v.shape[:-1] + (-1, 32))
    amax = np.abs(blocks).max(-1, keepdims=True)
    byte = np.maximum(np.where(amax > 0, np.frexp(amax)[1] - 1 + 127, 0) - down, 1)
    scale = np.exp2(byte - 127.0)
    codes = (blocks / scale).astype(np.float32).astype(dtype).astype(np.float64)
    return np.moveaxis((codes * scale).reshape(v.shape), -1, axis)


WIDE = False


def mx_kscale(k, group=512):
    if not WIDE:
        return np.ones(k)
    levels = np.array([10, -10, 5, -5, 0])
    if group != 512:
        return np.exp2(np.random.permutation(np.resize(levels, k // group))).repeat(group)
    if k % 512:
        return np.exp2(np.random.permutation(np.resize(levels, k // 32))).repeat(32)
    a = np.empty((k // 512, 16))
    for p in range(k // 512):
        a[p, :8] = np.random.permutation(np.resize(levels, 8))
        for g in range(8):
            far = levels[np.abs(levels - a[p, g]) >= 10]
            a[p, g + 8] = far[np.random.randint(len(far))]
    return np.exp2(a.ravel()).repeat(32)


def f64(x):
    return np.asarray(x).astype(np.float64)


H, D, N = 8, 256, 512


def setup_inputs():
    n = np.random.standard_normal
    s = mx_kscale(D, 0)
    u = mx_kscale(N)
    t = np.random.uniform(0.5, 2.0, N) * u
    v = n((H, N, 128))
    v[:, :, 127] = 1.0
    return {
        "q": n((H, D, N)).astype(np.float32),
        "qa": (np.random.uniform(0.5, 2.0, D) * s)[:, None].astype(np.float32),
        "ka": np.tile(np.random.uniform(0.5, 2.0, D) / s, (128, 1)).astype(np.float32),
        "k": n((H, N, D)).astype(np.float32),
        "t": t.reshape(N, 1).astype(np.float32),
        "v": (v / t[:, None]).astype(np.float32),
    }


def reference(q, qa, ka, k, t, v):
    fq = (np.square(f64(q)) + 0.125) * f64(qa)
    fk = (np.square(f64(k)) + 0.125) * f64(t) * f64(ka)[:1]
    S = (mxq(fk, 1, "e4m3").transpose(0, 2, 1) @ mxq(f64(v), 1, "e4m3")) / N
    y = mxq(fq, 1, "e4m3").transpose(0, 2, 1) @ mxq(S, 1, "e4m3")
    y = y / y[:, :, 127:128]
    return y

@@ -1,0 +1,210 @@
+from contextlib import ExitStack
+
+import concourse.mybir as mybir
+
+H, D, N, E = 8, 256, 512, 128
+FLOPS = 2 * 2 * H * N * D * E
+F32 = mybir.dt.float32
+BF16 = mybir.dt.bfloat16
+U32 = mybir.dt.uint32
+U8 = mybir.dt.uint8
+FP8X4 = mybir.dt.float8_e4m3fn_x4
+ACT = mybir.ActivationFunctionType
+ALU = mybir.AluOpType
+P = 128
+ORDER = "WU MS SK0a TK SK0b SK1a SK1b VK0a SK2a VK0b SK2b SQ0a VK1a VK1b VK2a QK0 VV0 SQ0b VK2b VQ0a SK3a QV0 SK3b QQ0a VV1 SQ1a VQ0b M10 VK3 SC0 SK4a SK4b SK5a QV1 QK1 M11 SK5b SC1 QQ0b VQ1a QS0 QQ1a SQ1b SQ2a M20 SQ2b VK4 VV2 VK5 QS1 QK2 QV2 SK6a SK6b R0 VQ1b M12 VQ2a SC2 SK7a QQ1b QQ2a VQ2b EV0 M21 R2 QQ2b R3 SK7b QS2 VK6 ST0 VK7 EV2 VV3 SQ3a R1 QK3 M22 QV3 ST2 EV3 SQ3b VQ3a R4 M13 EV1 R5 SC3 ST3 ST1 VQ3b QQ3a QS3 EV4 M23a QQ3b R6a ST4 M23b R7a EV5 EV6a R6b R7b ST5 EV7b EV7a EV6b ST6a ST7a ST6b ST7b".split()
+LOADS = "t ka k0a k0b k1 qa k2 q0a v0 q0b k3 v1 q1a q1b k4 k5 v2 q2a q2b k6 k7 v3 q3a q3b".split()
+ON_VECTOR = "EV7b EV6a".split()
+ON_SCALAR = "VV1".split()
+
+
+def tile_rows_lin_sq_norm_kernel(tc, q, qa, ka, k, t, v, out):
+    nc = tc.nc
+    with ExitStack() as ctx:
+        sb = ctx.enter_context(tc.tile_pool(name="sb", bufs=1))
+        ps = ctx.enter_context(tc.psum_pool(name="ps", bufs=1))
+
+        def tiles(name, count, shape, dtype):
+            return [sb.tile(shape, dtype, name="%s%d" % (name, i), align_bytes=64) for i in range(count)]
+
+        t_sb = sb.tile([P, 4], F32, name="t_sb")
+        qa_sb = sb.tile([P, 4], F32, name="qa_sb")
+        ka_sb = sb.tile([P, D], F32, name="ka_sb")
+        tk = sb.tile([P, 4, 64, 4], F32, name="tk", align_bytes=64)
+        warm = sb.tile([P, 2], F32, name="warm")
+        k_raw = tiles("k_raw", 8, [P, 4, D], F32)
+        k_sq = tiles("k_sq", 6, [P, 4, 64, 4], F32)
+        fk = tiles("fk", 4, [P, 4, 2, 256], BF16)
+        k_codes = sb.tile([P, 4 * 768], U32, name="k_codes", align_bytes=64)
+        k_scales = sb.tile([P, 4 * 768], U8, name="k_scales", align_bytes=64)
+        v_raw = tiles("v_raw", 4, [P, 2, 4, E], F32)
+        v_bf = tiles("v_bf", 4, [P, 2, E, 4], BF16)
+        v_codes = tiles("v_codes", 4, [P, 256], U32)
+        v_scales = tiles("v_scales", 4, [P, 256], U8)
+        q_raw = tiles("q_raw", 8, [P, 4, 256], F32)
+        q_sq = tiles("q_sq", 6, [P, 2, 128, 4], F32)
+        fq = tiles("fq", 8, [P, 256, 4], BF16)
+        q_codes = tiles("q_codes", 8, [P, 256], U32)
+        q_scales = tiles("q_scales", 8, [P, 256], U8)
+        s_bf = tiles("s_bf", 4, [P, E, 4], BF16)
+        s_codes = tiles("s_codes", 4, [P, E], U32)
+        s_scales = tiles("s_scales", 4, [P, E], U8)
+        rec = tiles("rec", 16, [P, 4], F32)
+        res = tiles("res", 8, [P, 4, E], F32)
+        state = [ps.tile([P, 4, E], F32, name="state%d" % i) for i in range(2)]
+        ybank = [[ps.tile([P, 4, E], F32, name="y%d_%d" % (c, i)) for i in range(3)] for c in range(2)]
+
+        def load(name):
+            if name == "t":
+                nc.sync.dma_start(out=t_sb[:], in_=t.rearrange("(p j) o -> p (j o)", j=4))
+            elif name == "ka":
+                nc.sync.dma_start(out=ka_sb[:], in_=ka)
+            elif name == "qa":
+                for c in range(2):
+                    nc.sync.dma_start(out=qa_sb[64 * c : 64 * c + 64, :], in_=qa.rearrange("(p j) o -> p (j o)", j=4))
+            elif name[0] == "k":
+                h = int(name[1])
+                cols = slice(0, D) if len(name) == 2 else slice(128 * "ab".index(name[2]), 128 * "ab".index(name[2]) + 128)
+                nc.sync.dma_start(out=k_raw[h][:, :, cols], in_=k[h].rearrange("(p j) d -> p j d", j=4)[:, :, cols])
+            elif name[0] == "v":
+                g = int(name[1])
+                nc.sync.dma_start(out=v_raw[g][:], in_=v[2 * g : 2 * g + 2].rearrange("c (p j) e -> p c j e", j=4))
+            else:
+                g, a = int(name[1]), "ab".index(name[2])
+                nc.sync.dma_start(
+                    out=q_raw[2 * g + a][:],
+                    in_=q[2 * g : 2 * g + 2].rearrange("c (p j) n -> (c p) j n", j=4)[:, :, 256 * a : 256 * a + 256],
+                )
+
+        def quant(codes, scales, src):
+            nc.vector.quantize_mx(out=codes.bitcast(FP8X4), scales=scales, in_=src)
+
+        def mm(dst, lc, ls, rc, rs, start, stop):
+            nc.tensor.matmul_mx(out=dst, lhsT=lc.bitcast(FP8X4), lhsT_scale=ls, rhs=rc.bitcast(FP8X4), rhs_scale=rs, start=start, stop=stop)
+
+        def bank(h, a):
+            g, c = divmod(h, 2)
+            return ybank[c][(g + (a or 0)) % 3]
+
+        def slots(a):
+            return slice(0, 4) if a is None else slice(2 * a, 2 * a + 2)
+
+        def run(name):
+            op = name[:2] if name[0] != "R" else "R"
+            rest = name[len(op):]
+            i = int(rest[0]) if rest else 0
+            a = "ab".index(rest[1]) if len(rest) > 1 else None
+            if op == "WU":
+                nc.vector.memset(warm[:, 0:1], 0.0)
+                nc.scalar.activation(out=warm[:, 1:2], in_=warm[:, 0:1], func=ACT.Square)
+            elif op == "MS":
+                nc.vector.memset(k_codes[:].rearrange("p (b w) -> p b w", w=192)[:, :, 64:128], 0)
+                nc.vector.memset(k_scales[:].bitcast(U32).rearrange("p (b w) -> p b w", w=48)[:, :, 16:32], 0x01010101)
+            elif op == "TK":
+                nc.vector.tensor_tensor(
+                    out=tk[:],
+                    in0=ka_sb[:].rearrange("p (m x) -> p x m", x=4).unsqueeze(3).to_broadcast([P, 4, 64, 4]),
+                    in1=t_sb[:].unsqueeze(1).unsqueeze(1).to_broadcast([P, 4, 64, 4]),
+                    op=ALU.mult,
+                )
+            elif op == "SK":
+                src = k_raw[i][:].rearrange("p j (m x) -> p m j x", x=4)
+                dst = k_sq[i % 6][:].rearrange("p x m j -> p m j x")
+                if a is None:
+                    nc.scalar.activation(out=dst, in_=src, func=ACT.Square)
+                elif i == 0:
+                    nc.scalar.activation(out=dst[:, 32 * a : 32 * a + 32], in_=src[:, 32 * a : 32 * a + 32], func=ACT.Square)
+                else:
+                    nc.scalar.activation(out=dst[:, :, :, 2 * a : 2 * a + 2], in_=src[:, :, :, 2 * a : 2 * a + 2], func=ACT.Square)
+            elif op == "VK":
+                g, c = divmod(i, 2)
+                dst = fk[g][:, :, c, :]
+                src = k_sq[i % 6][:].rearrange("p x m j -> p x (m j)")
+                fac = tk[:].rearrange("p x m j -> p x (m j)")
+                if a is not None and i == 0:
+                    dst, src, fac = [w[:, :, 128 * a : 128 * a + 128] for w in (dst, src, fac)]
+                elif a is not None:
+                    dst, src, fac = [w[:, 2 * a : 2 * a + 2, :] for w in (dst, src, fac)]
+                nc.vector.scalar_tensor_tensor(out=dst, in0=src, scalar=0.125, in1=fac, op0=ALU.add, op1=ALU.mult)
+            elif op == "QK":
+                flat = fk[i][:].rearrange("p x c w -> p (x c w)")
+                for first, width, word in ((0, 256, 0), (256, 512, 128), (768, 512, 320), (1280, 512, 512), (1792, 256, 704)):
+                    w = slice(768 * i + word, 768 * i + word + width // 4)
+                    quant(k_codes[:, w], k_scales[:, w], flat[:, first : first + width])
+            elif op == "VV":
+                dst = v_bf[i][:].rearrange("p c (f u) j -> p c f j u", u=4)
+                src = v_raw[i][:].rearrange("p c j (f u) -> p c f j u", u=4)
+                if name in ON_SCALAR:
+                    for c in range(2):
+                        nc.scalar.copy(out=dst[:, c], in_=src[:, c])
+                else:
+                    nc.vector.tensor_copy(out=dst, in_=src)
+            elif op == "QV":
+                quant(v_codes[i][:], v_scales[i][:], v_bf[i][:].rearrange("p c e j -> p (c e j)"))
+            elif op == "SQ":
+                u = 2 * i + a
+                nc.scalar.activation(
+                    out=q_sq[u % 6][:].rearrange("p r m j -> p m j r"),
+                    in_=q_raw[u][:].rearrange("p j (m r) -> p m j r", r=2),
+                    func=ACT.Square,
+                )
+            elif op == "VQ":
+                u = 2 * i + a
+                nc.vector.scalar_tensor_tensor(
+                    out=fq[u][:],
+                    in0=q_sq[u % 6][:].rearrange("p r m j -> p (r m) j"),
+                    scalar=0.125,
+                    in1=qa_sb[:].unsqueeze(1).to_broadcast([P, 256, 4]),
+                    op0=ALU.add,
+                    op1=ALU.mult,
+                )
+            elif op == "QQ":
+                u = 2 * i + a
+                quant(q_codes[u][:], q_scales[u][:], fq[u][:].rearrange("p n j -> p (n j)"))
+            elif op == "M1":
+                for x in range(4):
+                    for c in range(2):
+                        w = slice(768 * i + 192 * x + 64 * c, 768 * i + 192 * x + 64 * c + 128)
+                        e = slice(128 * c, 128 * c + 128)
+                        mm(state[i % 2][:, x, :], k_codes[:, w], k_scales[:, w], v_codes[i][:, e], v_scales[i][:, e], c == 0, c == 1)
+            elif op == "SC":
+                src = state[i % 2][:].rearrange("p x e -> p e x")
+                if name in ON_VECTOR:
+                    nc.vector.tensor_scalar(out=s_bf[i][:], in0=src, scalar1=1.0 / N, scalar2=None, op0=ALU.mult)
+                else:
+                    nc.scalar.activation(out=s_bf[i][:], in_=src, func=ACT.Copy, scale=1.0 / N)
+            elif op == "QS":
+                quant(s_codes[i][:], s_scales[i][:], s_bf[i][:].rearrange("p e x -> p (e x)"))
+            elif op == "M2":
+                for s in range(4)[slots(a)]:
+                    for c in range(2):
+                        rows = slice(64 * c, 64 * c + 64)
+                        u = 2 * i + s // 2
+                        m = slice(128 * (s % 2), 128 * (s % 2) + 128)
+                        mm(bank(2 * i + c, a)[:, s, :], q_codes[u][rows, m], q_scales[u][rows, m], s_codes[i][rows, :], s_scales[i][rows, :], True, True)
+            elif op == "R":
+                nc.vector.reciprocal(out=rec[2 * i + (a or 0)][:, slots(a)], in_=bank(i, a)[:, slots(a), E - 1])
+            elif op == "EV":
+                r = rec[2 * i + (a or 0)]
+                if name in ON_VECTOR:
+                    n = 4 if a is None else 2
+                    nc.vector.tensor_tensor(
+                        out=res[i][:, slots(a), :], in0=bank(i, a)[:, slots(a), :],
+                        in1=r[:, slots(a)].unsqueeze(2).to_broadcast([P, n, E]), op=ALU.mult,
+                    )
+                else:
+                    for s in range(4)[slots(a)]:
+                        nc.scalar.activation(out=res[i][:, s, :], in_=bank(i, a)[:, s, :], func=ACT.Copy, scale=r[:, s : s + 1])
+            elif op == "ST":
+                dst = out[i].rearrange("(a m r) e -> m a (r e)", a=2, r=2)
+                src = res[i][:].rearrange("p (a r) e -> p a (r e)", a=2)
+                if a is None:
+                    nc.sync.dma_start(out=dst, in_=src)
+                else:
+                    nc.sync.dma_start(out=dst[:, a, :], in_=src[:, a, :])
+
+        with tc.manual_schedule():
+            for name in LOADS:
+                load(name)
+            for name in ORDER:
+                run(name)

@@ -12,9 +12,9 @@ FP8X4 = mybir.dt.float8_e4m3fn_x4
 ACT = mybir.ActivationFunctionType
 ALU = mybir.AluOpType
 P = 128
-ORDER = "WU MS SK0a TK SK0b SK1a SK1b VK0a SK2a VK0b SK2b SQ0a VK1a VK1b VK2a QK0 VV0 SQ0b VK2b VQ0a SK3a QV0 SK3b QQ0a VV1 SQ1a VQ0b M10 VK3 SC0 SK4a SK4b SK5a QV1 QK1 M11 SK5b SC1 QQ0b VQ1a QS0 QQ1a SQ1b SQ2a M20 SQ2b VK4 VV2 VK5 QS1 QK2 QV2 SK6a SK6b R0 VQ1b M12 VQ2a SC2 SK7a QQ1b QQ2a VQ2b EV0 M21 R2 QQ2b R3 SK7b QS2 VK6 ST0 VK7 EV2 VV3 SQ3a R1 QK3 M22 QV3 ST2 EV3 SQ3b VQ3a R4 M13 EV1 R5 SC3 ST3 ST1 VQ3b QQ3a QS3 EV4 M23a QQ3b R6a ST4 M23b R7a EV5 EV6a R6b R7b ST5 EV7b EV7a EV6b ST6a ST7a ST6b ST7b".split()
-LOADS = "t ka k0a k0b k1 qa k2 q0a v0 q0b k3 v1 q1a q1b k4 k5 v2 q2a q2b k6 k7 v3 q3a q3b".split()
-ON_VECTOR = "EV7b EV6a".split()
+ORDER = "WU MS SK0a TK SK0b SK1a SK1b VK0a VK0b SQ0a VK1a SQ0b VK1b QK0 SK2a VV0 SK2b VQ0a SK3a QV0 VQ0b QQ0a SK3b VK2a M10 VK3 SC0 VV1 QQ0b QS0 QV1 SQ1a VK2b SQ1b M20 R0 SK4a QK1 VQ1a M11 VQ1b R1 VV2 QQ1a QQ1b EV0 SC1 SK4b QS1 QV2 EV1 SK5a VK4 M21 R2 SK5b R3 VV3 EV2 SK6a VK5 SK6b QV3 SK7a QK2 VK6 SK7b M12 VK7 SQ2a EV3 VQ2a SQ2b SC2 ST0 QK3 ST1 M13 QQ2a VQ2b SQ3a QS2 SQ3b QQ2b ST2 VQ3a M22 R4 SC3 R5 VQ3c EV4 QS3 ST3 QQ3a VQ3d EV5 QQ3c ST4 M23a ST5 R6a R7a M23c EV6a QQ3d EV7a R7c M23d R6c EV7c R6d EV6c R7d ST3a EV6d EV7d ST3c ST3d".split()
+LOADS = "k0 ka t qa k1 q0 v0 k2 k3 v1 q1 v2 k4 k5 v3 k6 k7 q2 q3".split()
+ON_VECTOR = "EV7a EV7d EV6d".split()
 ON_SCALAR = "VV1".split()
 
 
@@ -41,7 +41,7 @@ def tile_rows_lin_sq_norm_kernel(tc, q, qa, ka, k, t, v, out):
         v_bf = tiles("v_bf", 4, [P, 2, E, 4], BF16)
         v_codes = tiles("v_codes", 4, [P, 256], U32)
         v_scales = tiles("v_scales", 4, [P, 256], U8)
-        q_raw = tiles("q_raw", 8, [P, 4, 256], F32)
+        q_raw = tiles("q_raw", 4, [P, 4, N], F32)
         q_sq = tiles("q_sq", 6, [P, 2, 128, 4], F32)
         fq = tiles("fq", 8, [P, 256, 4], BF16)
         q_codes = tiles("q_codes", 8, [P, 256], U32)
@@ -49,19 +49,19 @@ def tile_rows_lin_sq_norm_kernel(tc, q, qa, ka, k, t, v, out):
         s_bf = tiles("s_bf", 4, [P, E, 4], BF16)
         s_codes = tiles("s_codes", 4, [P, E], U32)
         s_scales = tiles("s_scales", 4, [P, E], U8)
-        rec = tiles("rec", 16, [P, 4], F32)
-        res = tiles("res", 8, [P, 4, E], F32)
+        rec = tiles("rec", 24, [P, 4], F32)
+        res = tiles("res", 4, [P, 2, 4, E], F32)
         state = [ps.tile([P, 4, E], F32, name="state%d" % i) for i in range(2)]
         ybank = [[ps.tile([P, 4, E], F32, name="y%d_%d" % (c, i)) for i in range(3)] for c in range(2)]
 
         def load(name):
             if name == "t":
-                nc.sync.dma_start(out=t_sb[:], in_=t.rearrange("(p j) o -> p (j o)", j=4))
+                nc.scalar.dma_start(out=t_sb[:], in_=t.rearrange("(p j) o -> p (j o)", j=4))
             elif name == "ka":
-                nc.sync.dma_start(out=ka_sb[:], in_=ka)
+                nc.scalar.dma_start(out=ka_sb[:], in_=ka)
             elif name == "qa":
                 for c in range(2):
-                    nc.sync.dma_start(out=qa_sb[64 * c : 64 * c + 64, :], in_=qa.rearrange("(p j) o -> p (j o)", j=4))
+                    nc.scalar.dma_start(out=qa_sb[64 * c : 64 * c + 64, :], in_=qa.rearrange("(p j) o -> p (j o)", j=4))
             elif name[0] == "k":
                 h = int(name[1])
                 cols = slice(0, D) if len(name) == 2 else slice(128 * "ab".index(name[2]), 128 * "ab".index(name[2]) + 128)
@@ -70,11 +70,8 @@ def tile_rows_lin_sq_norm_kernel(tc, q, qa, ka, k, t, v, out):
                 g = int(name[1])
                 nc.sync.dma_start(out=v_raw[g][:], in_=v[2 * g : 2 * g + 2].rearrange("c (p j) e -> p c j e", j=4))
             else:
-                g, a = int(name[1]), "ab".index(name[2])
-                nc.sync.dma_start(
-                    out=q_raw[2 * g + a][:],
-                    in_=q[2 * g : 2 * g + 2].rearrange("c (p j) n -> (c p) j n", j=4)[:, :, 256 * a : 256 * a + 256],
-                )
+                g = int(name[1])
+                nc.sync.dma_start(out=q_raw[g][:], in_=q[2 * g : 2 * g + 2].rearrange("c (p j) n -> (c p) j n", j=4))
 
         def quant(codes, scales, src):
             nc.vector.quantize_mx(out=codes.bitcast(FP8X4), scales=scales, in_=src)
@@ -82,18 +79,21 @@ def tile_rows_lin_sq_norm_kernel(tc, q, qa, ka, k, t, v, out):
         def mm(dst, lc, ls, rc, rs, start, stop):
             nc.tensor.matmul_mx(out=dst, lhsT=lc.bitcast(FP8X4), lhsT_scale=ls, rhs=rc.bitcast(FP8X4), rhs_scale=rs, start=start, stop=stop)
 
-        def bank(h, a):
+        def bank(h, part):
             g, c = divmod(h, 2)
-            return ybank[c][(g + (a or 0)) % 3]
+            return ybank[c][{"": g, "a": 0, "c": 1, "d": 2}[part]]
 
-        def slots(a):
-            return slice(0, 4) if a is None else slice(2 * a, 2 * a + 2)
+        def slots(part):
+            return {"": slice(0, 4), "a": slice(0, 2), "b": slice(2, 4), "c": slice(2, 3), "d": slice(3, 4)}[part]
 
         def run(name):
             op = name[:2] if name[0] != "R" else "R"
             rest = name[len(op):]
             i = int(rest[0]) if rest else 0
-            a = "ab".index(rest[1]) if len(rest) > 1 else None
+            part = rest[1:]
+            a = {"": None, "a": 0, "b": 1, "c": 1, "d": 1}[part]
+            sl = slots(part)
+            n = sl.stop - sl.start
             if op == "WU":
                 nc.vector.memset(warm[:, 0:1], 0.0)
                 nc.scalar.activation(out=warm[:, 1:2], in_=warm[:, 0:1], func=ACT.Square)
@@ -112,8 +112,6 @@ def tile_rows_lin_sq_norm_kernel(tc, q, qa, ka, k, t, v, out):
                 dst = k_sq[i % 6][:].rearrange("p x m j -> p m j x")
                 if a is None:
                     nc.scalar.activation(out=dst, in_=src, func=ACT.Square)
-                elif i == 0:
-                    nc.scalar.activation(out=dst[:, 32 * a : 32 * a + 32], in_=src[:, 32 * a : 32 * a + 32], func=ACT.Square)
                 else:
                     nc.scalar.activation(out=dst[:, :, :, 2 * a : 2 * a + 2], in_=src[:, :, :, 2 * a : 2 * a + 2], func=ACT.Square)
             elif op == "VK":
@@ -121,9 +119,7 @@ def tile_rows_lin_sq_norm_kernel(tc, q, qa, ka, k, t, v, out):
                 dst = fk[g][:, :, c, :]
                 src = k_sq[i % 6][:].rearrange("p x m j -> p x (m j)")
                 fac = tk[:].rearrange("p x m j -> p x (m j)")
-                if a is not None and i == 0:
-                    dst, src, fac = [w[:, :, 128 * a : 128 * a + 128] for w in (dst, src, fac)]
-                elif a is not None:
+                if a is not None:
                     dst, src, fac = [w[:, 2 * a : 2 * a + 2, :] for w in (dst, src, fac)]
                 nc.vector.scalar_tensor_tensor(out=dst, in0=src, scalar=0.125, in1=fac, op0=ALU.add, op1=ALU.mult)
             elif op == "QK":
@@ -145,22 +141,24 @@ def tile_rows_lin_sq_norm_kernel(tc, q, qa, ka, k, t, v, out):
                 u = 2 * i + a
                 nc.scalar.activation(
                     out=q_sq[u % 6][:].rearrange("p r m j -> p m j r"),
-                    in_=q_raw[u][:].rearrange("p j (m r) -> p m j r", r=2),
+                    in_=q_raw[i][:].rearrange("p j (m r) -> p m j r", r=4)[:, :, :, sl],
                     func=ACT.Square,
                 )
             elif op == "VQ":
                 u = 2 * i + a
+                cols = slice(128 * (sl.start % 2), 128 * (sl.start % 2) + 128 * n)
                 nc.vector.scalar_tensor_tensor(
-                    out=fq[u][:],
-                    in0=q_sq[u % 6][:].rearrange("p r m j -> p (r m) j"),
+                    out=fq[u][:, cols, :],
+                    in0=q_sq[u % 6][:].rearrange("p r m j -> p (r m) j")[:, cols, :],
                     scalar=0.125,
-                    in1=qa_sb[:].unsqueeze(1).to_broadcast([P, 256, 4]),
+                    in1=qa_sb[:].unsqueeze(1).to_broadcast([P, 128 * n, 4]),
                     op0=ALU.add,
                     op1=ALU.mult,
                 )
             elif op == "QQ":
                 u = 2 * i + a
-                quant(q_codes[u][:], q_scales[u][:], fq[u][:].rearrange("p n j -> p (n j)"))
+                cols = slice(128 * (sl.start % 2), 128 * (sl.start % 2) + 128 * n)
+                quant(q_codes[u][:, cols], q_scales[u][:, cols], fq[u][:, cols, :].rearrange("p n j -> p (n j)"))
             elif op == "M1":
                 for x in range(4):
                     for c in range(2):
@@ -176,32 +174,33 @@ def tile_rows_lin_sq_norm_kernel(tc, q, qa, ka, k, t, v, out):
             elif op == "QS":
                 quant(s_codes[i][:], s_scales[i][:], s_bf[i][:].rearrange("p e x -> p (e x)"))
             elif op == "M2":
-                for s in range(4)[slots(a)]:
+                for s in range(sl.start, sl.stop):
                     for c in range(2):
                         rows = slice(64 * c, 64 * c + 64)
                         u = 2 * i + s // 2
                         m = slice(128 * (s % 2), 128 * (s % 2) + 128)
-                        mm(bank(2 * i + c, a)[:, s, :], q_codes[u][rows, m], q_scales[u][rows, m], s_codes[i][rows, :], s_scales[i][rows, :], True, True)
+                        mm(bank(2 * i + c, part)[:, s, :], q_codes[u][rows, m], q_scales[u][rows, m], s_codes[i][rows, :], s_scales[i][rows, :], True, True)
             elif op == "R":
-                nc.vector.reciprocal(out=rec[2 * i + (a or 0)][:, slots(a)], in_=bank(i, a)[:, slots(a), E - 1])
+                r = rec[3 * i + {"": 0, "a": 0, "c": 1, "d": 2}[part]]
+                nc.vector.reciprocal(out=r[:, sl], in_=bank(i, part)[:, sl, E - 1])
             elif op == "EV":
-                r = rec[2 * i + (a or 0)]
+                r = rec[3 * i + {"": 0, "a": 0, "c": 1, "d": 2}[part]]
+                dst = res[i // 2][:, i % 2]
                 if name in ON_VECTOR:
-                    n = 4 if a is None else 2
                     nc.vector.tensor_tensor(
-                        out=res[i][:, slots(a), :], in0=bank(i, a)[:, slots(a), :],
-                        in1=r[:, slots(a)].unsqueeze(2).to_broadcast([P, n, E]), op=ALU.mult,
+                        out=dst[:, sl, :], in0=bank(i, part)[:, sl, :],
+                        in1=r[:, sl].unsqueeze(2).to_broadcast([P, n, E]), op=ALU.mult,
                     )
                 else:
-                    for s in range(4)[slots(a)]:
-                        nc.scalar.activation(out=res[i][:, s, :], in_=bank(i, a)[:, s, :], func=ACT.Copy, scale=r[:, s : s + 1])
+                    for s in range(sl.start, sl.stop):
+                        nc.scalar.activation(out=dst[:, s, :], in_=bank(i, part)[:, s, :], func=ACT.Copy, scale=r[:, s : s + 1])
             elif op == "ST":
-                dst = out[i].rearrange("(a m r) e -> m a (r e)", a=2, r=2)
-                src = res[i][:].rearrange("p (a r) e -> p a (r e)", a=2)
-                if a is None:
-                    nc.sync.dma_start(out=dst, in_=src)
+                if part == "":
+                    nc.sync.dma_start(out=out[i].rearrange("(m r) e -> m r e", r=4), in_=res[i // 2][:, i % 2])
                 else:
-                    nc.sync.dma_start(out=dst[:, a, :], in_=src[:, a, :])
+                    nc.sync.dma_start(
+                        out=out[2 * i : 2 * i + 2].rearrange("c (m r) e -> m c r e", r=4)[:, :, sl, :], in_=res[i][:, :, sl, :]
+                    )
 
         with tc.manual_schedule():
             for name in LOADS:

@@ -12,10 +12,10 @@ FP8X4 = mybir.dt.float8_e4m3fn_x4
 ACT = mybir.ActivationFunctionType
 ALU = mybir.AluOpType
 P = 128
-ORDER = "WU MS SK0a TK SK0b SK1a SK1b VK0a VK0b SQ0a VK1a SQ0b VK1b QK0 SK2a VV0 SK2b VQ0a SK3a QV0 VQ0b QQ0a SK3b VK2a M10 VK3 SC0 VV1 QQ0b QS0 QV1 SQ1a VK2b SQ1b M20 R0 SK4a QK1 VQ1a M11 VQ1b R1 VV2 QQ1a QQ1b EV0 SC1 SK4b QS1 QV2 EV1 SK5a VK4 M21 R2 SK5b R3 VV3 EV2 SK6a VK5 SK6b QV3 SK7a QK2 VK6 SK7b M12 VK7 SQ2a EV3 VQ2a SQ2b SC2 ST0 QK3 ST1 M13 QQ2a VQ2b SQ3a QS2 SQ3b QQ2b ST2 VQ3a M22 R4 SC3 R5 VQ3c EV4 QS3 ST3 QQ3a VQ3d EV5 QQ3c ST4 M23a ST5 R6a R7a M23c EV6a QQ3d EV7a R7c M23d R6c EV7c R6d EV6c R7d ST3a EV6d EV7d ST3c ST3d".split()
-LOADS = "k0 ka t qa k1 q0 v0 k2 k3 v1 q1 v2 k4 k5 v3 k6 k7 q2 q3".split()
-ON_VECTOR = "EV7a EV7d EV6d".split()
-ON_SCALAR = "VV1".split()
+ORDER = "WU MS SK0a SK0b SK1a SK1b VV0 SK2a SK2b SK3a SK3b TK VK0a VK0b VK1a VK1b QV0 QK0 VK2a VK2b VK3a VK3b M10 SC0 SQ0a SQ0b SQ1a SQ1b SK4a SK4b SK5a QS0 QK1 VQ0a VQ0b VV1 QQ0 QV1 VQ1 M11 M20 SC1 SK5b R0 R1 QS1 QQ1 VK4 M21 EV0 EV1 SK6a R2 VK5 VV2 R3 QK2 ST0 ST1 EV2 SK6b SK7a SK7b SQ2a SQ2b VV3 VK6 VK7 QV2 QK3 VQ2 QV3 M12 M13 ST2 SC2 SQ3a SQ3b EV3 SC3 QS2 QQ2 VQ3a VQ3c M22 ST3 R4 QQ3a QS3 R5 VQ3d QQ3c M23a M23c EV4 EV5 R6a R7a QQ3d EV6a R6c R7c M23d ST4 ST5 EV7a EV6c EV7c R6d R7d EV7d ST3a ST3c EV6d ST3d".split()
+LOADS = "k0 ka t k1 v0 k2 k3 q0 qa q1 v1 k4 k5 k6 v2 k7 q2 v3 q3".split()
+ON_VECTOR = "EV6a EV7d".split()
+ON_SCALAR = "VV0 VV3".split()
 
 
 def tile_rows_lin_sq_norm_kernel(tc, q, qa, ka, k, t, v, out):
@@ -42,10 +42,10 @@ def tile_rows_lin_sq_norm_kernel(tc, q, qa, ka, k, t, v, out):
         v_codes = tiles("v_codes", 4, [P, 256], U32)
         v_scales = tiles("v_scales", 4, [P, 256], U8)
         q_raw = tiles("q_raw", 4, [P, 4, N], F32)
-        q_sq = tiles("q_sq", 6, [P, 2, 128, 4], F32)
-        fq = tiles("fq", 8, [P, 256, 4], BF16)
-        q_codes = tiles("q_codes", 8, [P, 256], U32)
-        q_scales = tiles("q_scales", 8, [P, 256], U8)
+        q_sq = tiles("q_sq", 3, [P, 4, 128, 4], F32)
+        fq = tiles("fq", 4, [P, N, 4], BF16)
+        q_codes = tiles("q_codes", 4, [P, N], U32)
+        q_scales = tiles("q_scales", 4, [P, N], U8)
         s_bf = tiles("s_bf", 4, [P, E, 4], BF16)
         s_codes = tiles("s_codes", 4, [P, E], U32)
         s_scales = tiles("s_scales", 4, [P, E], U8)
@@ -56,12 +56,12 @@ def tile_rows_lin_sq_norm_kernel(tc, q, qa, ka, k, t, v, out):
 
         def load(name):
             if name == "t":
-                nc.scalar.dma_start(out=t_sb[:], in_=t.rearrange("(p j) o -> p (j o)", j=4))
+                nc.sync.dma_start(out=t_sb[:], in_=t.rearrange("(p j) o -> p (j o)", j=4))
             elif name == "ka":
-                nc.scalar.dma_start(out=ka_sb[:], in_=ka)
+                nc.sync.dma_start(out=ka_sb[:], in_=ka)
             elif name == "qa":
                 for c in range(2):
-                    nc.scalar.dma_start(out=qa_sb[64 * c : 64 * c + 64, :], in_=qa.rearrange("(p j) o -> p (j o)", j=4))
+                    nc.sync.dma_start(out=qa_sb[64 * c : 64 * c + 64, :], in_=qa.rearrange("(p j) o -> p (j o)", j=4))
             elif name[0] == "k":
                 h = int(name[1])
                 cols = slice(0, D) if len(name) == 2 else slice(128 * "ab".index(name[2]), 128 * "ab".index(name[2]) + 128)
@@ -138,27 +138,24 @@ def tile_rows_lin_sq_norm_kernel(tc, q, qa, ka, k, t, v, out):
             elif op == "QV":
                 quant(v_codes[i][:], v_scales[i][:], v_bf[i][:].rearrange("p c e j -> p (c e j)"))
             elif op == "SQ":
-                u = 2 * i + a
                 nc.scalar.activation(
-                    out=q_sq[u % 6][:].rearrange("p r m j -> p m j r"),
+                    out=q_sq[i % 3][:].rearrange("p r m j -> p m j r")[:, :, :, sl],
                     in_=q_raw[i][:].rearrange("p j (m r) -> p m j r", r=4)[:, :, :, sl],
                     func=ACT.Square,
                 )
             elif op == "VQ":
-                u = 2 * i + a
-                cols = slice(128 * (sl.start % 2), 128 * (sl.start % 2) + 128 * n)
+                cols = slice(128 * sl.start, 128 * sl.stop)
                 nc.vector.scalar_tensor_tensor(
-                    out=fq[u][:, cols, :],
-                    in0=q_sq[u % 6][:].rearrange("p r m j -> p (r m) j")[:, cols, :],
+                    out=fq[i][:, cols, :],
+                    in0=q_sq[i % 3][:].rearrange("p r m j -> p (r m) j")[:, cols, :],
                     scalar=0.125,
                     in1=qa_sb[:].unsqueeze(1).to_broadcast([P, 128 * n, 4]),
                     op0=ALU.add,
                     op1=ALU.mult,
                 )
             elif op == "QQ":
-                u = 2 * i + a
-                cols = slice(128 * (sl.start % 2), 128 * (sl.start % 2) + 128 * n)
-                quant(q_codes[u][:, cols], q_scales[u][:, cols], fq[u][:, cols, :].rearrange("p n j -> p (n j)"))
+                cols = slice(128 * sl.start, 128 * sl.stop)
+                quant(q_codes[i][:, cols], q_scales[i][:, cols], fq[i][:, cols, :].rearrange("p n j -> p (n j)"))
             elif op == "M1":
                 for x in range(4):
                     for c in range(2):
@@ -177,8 +174,8 @@ def tile_rows_lin_sq_norm_kernel(tc, q, qa, ka, k, t, v, out):
                 for s in range(sl.start, sl.stop):
                     for c in range(2):
                         rows = slice(64 * c, 64 * c + 64)
-                        u = 2 * i + s // 2
-                        m = slice(128 * (s % 2), 128 * (s % 2) + 128)
+                        u = i
+                        m = slice(128 * s, 128 * s + 128)
                         mm(bank(2 * i + c, part)[:, s, :], q_codes[u][rows, m], q_scales[u][rows, m], s_codes[i][rows, :], s_scales[i][rows, :], True, True)
             elif op == "R":
                 r = rec[3 * i + {"": 0, "a": 0, "c": 1, "d": 2}[part]]

@@ -3,7 +3,8 @@ from contextlib import ExitStack
 import concourse.mybir as mybir
 
 H, D, N, E = 8, 256, 512, 128
-FLOPS = 2 * 2 * H * N * D * E
+FLOPS = 2 * (2 * H * N * D * E)
+
 F32 = mybir.dt.float32
 BF16 = mybir.dt.bfloat16
 U32 = mybir.dt.uint32
@@ -11,11 +12,23 @@ U8 = mybir.dt.uint8
 FP8X4 = mybir.dt.float8_e4m3fn_x4
 ACT = mybir.ActivationFunctionType
 ALU = mybir.AluOpType
+
 P = 128
-ORDER = "WU MS SK0a SK0b SK1a SK1b VV0 SK2a SK2b SK3a SK3b TK VK0a VK0b VK1a VK1b QV0 QK0 VK2a VK2b VK3a VK3b M10 SC0 SQ0a SQ0b SQ1a SQ1b SK4a SK4b SK5a QS0 QK1 VQ0a VQ0b VV1 QQ0 QV1 VQ1 M11 M20 SC1 SK5b R0 R1 QS1 QQ1 VK4 M21 EV0 EV1 SK6a R2 VK5 VV2 R3 QK2 ST0 ST1 EV2 SK6b SK7a SK7b SQ2a SQ2b VV3 VK6 VK7 QV2 QK3 VQ2 QV3 M12 M13 ST2 SC2 SQ3a SQ3b EV3 SC3 QS2 QQ2 VQ3a VQ3c M22 ST3 R4 QQ3a QS3 R5 VQ3d QQ3c M23a M23c EV4 EV5 R6a R7a QQ3d EV6a R6c R7c M23d ST4 ST5 EV7a EV6c EV7c R6d R7d EV7d ST3a ST3c EV6d ST3d".split()
-LOADS = "k0 ka t k1 v0 k2 k3 q0 qa q1 v1 k4 k5 k6 v2 k7 q2 v3 q3".split()
-ON_VECTOR = "EV6a EV7d".split()
-ON_SCALAR = "VV0 VV3".split()
+PACK = 4
+TILE = D // PACK
+PAIRS = H // 2
+GROUP = 3 * TILE
+PAIR_WORDS = PACK * GROUP
+PHI_SHIFT = 0.125
+SCALE_BYTES_ONE = 0x01010101
+
+KEY_SQUARE_BUFS = 6
+QUERY_SQUARE_BUFS = 3
+STATE_BANKS = 2
+ROW_TILE_BANKS = 3
+
+ALL_GROUPS = slice(0, PACK)
+LAST_PARTS = (slice(0, 2), slice(2, 3), slice(3, 4))
 
 
 def tile_rows_lin_sq_norm_kernel(tc, q, qa, ka, k, t, v, out):
@@ -27,180 +40,285 @@ def tile_rows_lin_sq_norm_kernel(tc, q, qa, ka, k, t, v, out):
         def tiles(name, count, shape, dtype):
             return [sb.tile(shape, dtype, name="%s%d" % (name, i), align_bytes=64) for i in range(count)]
 
-        t_sb = sb.tile([P, 4], F32, name="t_sb")
-        qa_sb = sb.tile([P, 4], F32, name="qa_sb")
+        t_sb = sb.tile([P, PACK], F32, name="t_sb")
+        qa_sb = sb.tile([P, PACK], F32, name="qa_sb")
         ka_sb = sb.tile([P, D], F32, name="ka_sb")
-        tk = sb.tile([P, 4, 64, 4], F32, name="tk", align_bytes=64)
-        warm = sb.tile([P, 2], F32, name="warm")
-        k_raw = tiles("k_raw", 8, [P, 4, D], F32)
-        k_sq = tiles("k_sq", 6, [P, 4, 64, 4], F32)
-        fk = tiles("fk", 4, [P, 4, 2, 256], BF16)
-        k_codes = sb.tile([P, 4 * 768], U32, name="k_codes", align_bytes=64)
-        k_scales = sb.tile([P, 4 * 768], U8, name="k_scales", align_bytes=64)
-        v_raw = tiles("v_raw", 4, [P, 2, 4, E], F32)
-        v_bf = tiles("v_bf", 4, [P, 2, E, 4], BF16)
-        v_codes = tiles("v_codes", 4, [P, 256], U32)
-        v_scales = tiles("v_scales", 4, [P, 256], U8)
-        q_raw = tiles("q_raw", 4, [P, 4, N], F32)
-        q_sq = tiles("q_sq", 3, [P, 4, 128, 4], F32)
-        fq = tiles("fq", 4, [P, N, 4], BF16)
-        q_codes = tiles("q_codes", 4, [P, N], U32)
-        q_scales = tiles("q_scales", 4, [P, N], U8)
-        s_bf = tiles("s_bf", 4, [P, E, 4], BF16)
-        s_codes = tiles("s_codes", 4, [P, E], U32)
-        s_scales = tiles("s_scales", 4, [P, E], U8)
-        rec = tiles("rec", 24, [P, 4], F32)
-        res = tiles("res", 4, [P, 2, 4, E], F32)
-        state = [ps.tile([P, 4, E], F32, name="state%d" % i) for i in range(2)]
-        ybank = [[ps.tile([P, 4, E], F32, name="y%d_%d" % (c, i)) for i in range(3)] for c in range(2)]
+        key_factor = sb.tile([P, PACK, TILE, PACK], F32, name="key_factor", align_bytes=64)
+        k_raw = tiles("k_raw", H, [P, PACK, D], F32)
+        k_sq = tiles("k_sq", KEY_SQUARE_BUFS, [P, 2, 2 * D], F32)
+        k_bf = tiles("k_bf", PAIRS, [P, PACK, 2, TILE * PACK], BF16)
+        k_codes = sb.tile([P, PAIRS * PAIR_WORDS], U32, name="k_codes", align_bytes=64)
+        k_scales = sb.tile([P, PAIRS * PAIR_WORDS], U8, name="k_scales", align_bytes=64)
+        v_raw = tiles("v_raw", PAIRS, [P, 2, PACK, E], F32)
+        v_bf = tiles("v_bf", PAIRS, [P, 2, E, PACK], BF16)
+        v_codes = tiles("v_codes", PAIRS, [P, 2 * E], U32)
+        v_scales = tiles("v_scales", PAIRS, [P, 2 * E], U8)
+        q_raw = tiles("q_raw", PAIRS, [P, PACK, N], F32)
+        q_sq = tiles("q_sq", QUERY_SQUARE_BUFS, [P, 2, 2 * N], F32)
+        q_bf = tiles("q_bf", PAIRS, [P, N, PACK], BF16)
+        q_codes = tiles("q_codes", PAIRS, [P, N], U32)
+        q_scales = tiles("q_scales", PAIRS, [P, N], U8)
+        s_bf = tiles("s_bf", PAIRS, [P, E, PACK], BF16)
+        s_codes = tiles("s_codes", PAIRS, [P, E], U32)
+        s_scales = tiles("s_scales", PAIRS, [P, E], U8)
+        inv = tiles("inv", H, [P, PACK], F32)
+        res = tiles("res", PAIRS, [P, 2, PACK, E], F32)
+        state = [ps.tile([P, PACK, E], F32, name="state%d" % i) for i in range(STATE_BANKS)]
+        y_banks = [[ps.tile([P, PACK, E], F32, name="y%d_%d" % (c, i)) for i in range(ROW_TILE_BANKS)] for c in range(2)]
 
-        def load(name):
-            if name == "t":
-                nc.sync.dma_start(out=t_sb[:], in_=t.rearrange("(p j) o -> p (j o)", j=4))
-            elif name == "ka":
-                nc.sync.dma_start(out=ka_sb[:], in_=ka)
-            elif name == "qa":
-                for c in range(2):
-                    nc.sync.dma_start(out=qa_sb[64 * c : 64 * c + 64, :], in_=qa.rearrange("(p j) o -> p (j o)", j=4))
-            elif name[0] == "k":
-                h = int(name[1])
-                cols = slice(0, D) if len(name) == 2 else slice(128 * "ab".index(name[2]), 128 * "ab".index(name[2]) + 128)
-                nc.sync.dma_start(out=k_raw[h][:, :, cols], in_=k[h].rearrange("(p j) d -> p j d", j=4)[:, :, cols])
-            elif name[0] == "v":
-                g = int(name[1])
-                nc.sync.dma_start(out=v_raw[g][:], in_=v[2 * g : 2 * g + 2].rearrange("c (p j) e -> p c j e", j=4))
-            else:
-                g = int(name[1])
-                nc.sync.dma_start(out=q_raw[g][:], in_=q[2 * g : 2 * g + 2].rearrange("c (p j) n -> (c p) j n", j=4))
+        def load_keys(h):
+            nc.sync.dma_start(out=k_raw[h][:], in_=k[h].rearrange("(p j) d -> p j d", j=PACK))
 
-        def quant(codes, scales, src):
+        def load_values(g):
+            nc.sync.dma_start(out=v_raw[g][:], in_=v[2 * g : 2 * g + 2].rearrange("c (p j) e -> p c j e", j=PACK))
+
+        def load_queries(g):
+            nc.sync.dma_start(out=q_raw[g][:], in_=q[2 * g : 2 * g + 2].rearrange("c (m x) n -> (c m) x n", x=PACK))
+
+        def quantise(codes, scales, src):
             nc.vector.quantize_mx(out=codes.bitcast(FP8X4), scales=scales, in_=src)
 
-        def mm(dst, lc, ls, rc, rs, start, stop):
-            nc.tensor.matmul_mx(out=dst, lhsT=lc.bitcast(FP8X4), lhsT_scale=ls, rhs=rc.bitcast(FP8X4), rhs_scale=rs, start=start, stop=stop)
+        def matmul(dst, lhs_codes, lhs_scales, rhs_codes, rhs_scales, start, stop):
+            nc.tensor.matmul_mx(
+                out=dst,
+                lhsT=lhs_codes.bitcast(FP8X4),
+                lhsT_scale=lhs_scales,
+                rhs=rhs_codes.bitcast(FP8X4),
+                rhs_scale=rhs_scales,
+                start=start,
+                stop=stop,
+            )
 
-        def bank(h, part):
+        def square(dst, raw, half):
+            rows = raw.rearrange("p (hi lo) (m g) -> p lo m g hi", lo=2, g=PACK)
+            if half is None:
+                cols = dst.rearrange("p lo (g m hi) -> p lo m g hi", g=PACK, hi=2)
+            else:
+                cols = dst.rearrange("p lo (a g m hi) -> p a lo m g hi", a=2, g=PACK, hi=2)[:, half]
+                width = cols.shape[2]
+                rows = rows[:, :, width * half : width * (half + 1)]
+            for lo in range(2):
+                nc.scalar.activation(out=cols[:, lo], in_=rows[:, lo], func=ACT.Square)
+
+        def squares_by_word(sq, half):
+            if half is None:
+                return sq.rearrange("p lo (g m hi) -> p g m hi lo", g=PACK, hi=2)
+            return sq.rearrange("p lo (a g m hi) -> p a g m hi lo", a=2, g=PACK, hi=2)[:, half]
+
+        def shift_and_weigh(dst, sq, factor):
+            nc.vector.scalar_tensor_tensor(out=dst, in0=sq, scalar=PHI_SHIFT, in1=factor, op0=ALU.add, op1=ALU.mult)
+
+        def square_keys(h, half=None):
+            square(k_sq[h % KEY_SQUARE_BUFS][:], k_raw[h][:], half)
+
+        def map_keys(h, half=None):
             g, c = divmod(h, 2)
-            return ybank[c][{"": g, "a": 0, "c": 1, "d": 2}[part]]
+            dst = k_bf[g][:, :, c, :].rearrange("p x (m hi lo) -> p x m hi lo", hi=2, lo=2)
+            factor = key_factor[:].rearrange("p x m (hi lo) -> p x m hi lo", lo=2)
+            if half is not None:
+                cols = slice(TILE // 2 * half, TILE // 2 * (half + 1))
+                dst, factor = dst[:, :, cols], factor[:, :, cols]
+            shift_and_weigh(dst, squares_by_word(k_sq[h % KEY_SQUARE_BUFS][:], half), factor)
 
-        def slots(part):
-            return {"": slice(0, 4), "a": slice(0, 2), "b": slice(2, 4), "c": slice(2, 3), "d": slice(3, 4)}[part]
+        def quantise_keys(g):
+            flat = k_bf[g][:].rearrange("p x c w -> p (x c w)")
+            heads = [(0, 1)] + [(2 * x + 1, 2) for x in range(PACK - 1)] + [(2 * PACK - 1, 1)]
+            for first, count in heads:
+                word = PAIR_WORDS * g + GROUP * (first // 2) + 2 * TILE * (first % 2)
+                words = slice(word, word + TILE * count)
+                quantise(k_codes[:, words], k_scales[:, words], flat[:, D * first : D * (first + count)])
 
-        def run(name):
-            op = name[:2] if name[0] != "R" else "R"
-            rest = name[len(op):]
-            i = int(rest[0]) if rest else 0
-            part = rest[1:]
-            a = {"": None, "a": 0, "b": 1, "c": 1, "d": 1}[part]
-            sl = slots(part)
-            n = sl.stop - sl.start
-            if op == "WU":
-                nc.vector.memset(warm[:, 0:1], 0.0)
-                nc.scalar.activation(out=warm[:, 1:2], in_=warm[:, 0:1], func=ACT.Square)
-            elif op == "MS":
-                nc.vector.memset(k_codes[:].rearrange("p (b w) -> p b w", w=192)[:, :, 64:128], 0)
-                nc.vector.memset(k_scales[:].bitcast(U32).rearrange("p (b w) -> p b w", w=48)[:, :, 16:32], 0x01010101)
-            elif op == "TK":
-                nc.vector.tensor_tensor(
-                    out=tk[:],
-                    in0=ka_sb[:].rearrange("p (m x) -> p x m", x=4).unsqueeze(3).to_broadcast([P, 4, 64, 4]),
-                    in1=t_sb[:].unsqueeze(1).unsqueeze(1).to_broadcast([P, 4, 64, 4]),
-                    op=ALU.mult,
-                )
-            elif op == "SK":
-                src = k_raw[i][:].rearrange("p j (m x) -> p m j x", x=4)
-                dst = k_sq[i % 6][:].rearrange("p x m j -> p m j x")
-                if a is None:
-                    nc.scalar.activation(out=dst, in_=src, func=ACT.Square)
-                else:
-                    nc.scalar.activation(out=dst[:, :, :, 2 * a : 2 * a + 2], in_=src[:, :, :, 2 * a : 2 * a + 2], func=ACT.Square)
-            elif op == "VK":
-                g, c = divmod(i, 2)
-                dst = fk[g][:, :, c, :]
-                src = k_sq[i % 6][:].rearrange("p x m j -> p x (m j)")
-                fac = tk[:].rearrange("p x m j -> p x (m j)")
-                if a is not None:
-                    dst, src, fac = [w[:, 2 * a : 2 * a + 2, :] for w in (dst, src, fac)]
-                nc.vector.scalar_tensor_tensor(out=dst, in0=src, scalar=0.125, in1=fac, op0=ALU.add, op1=ALU.mult)
-            elif op == "QK":
-                flat = fk[i][:].rearrange("p x c w -> p (x c w)")
-                for first, width, word in ((0, 256, 0), (256, 512, 128), (768, 512, 320), (1280, 512, 512), (1792, 256, 704)):
-                    w = slice(768 * i + word, 768 * i + word + width // 4)
-                    quant(k_codes[:, w], k_scales[:, w], flat[:, first : first + width])
-            elif op == "VV":
-                dst = v_bf[i][:].rearrange("p c (f u) j -> p c f j u", u=4)
-                src = v_raw[i][:].rearrange("p c j (f u) -> p c f j u", u=4)
-                if name in ON_SCALAR:
-                    for c in range(2):
-                        nc.scalar.copy(out=dst[:, c], in_=src[:, c])
-                else:
-                    nc.vector.tensor_copy(out=dst, in_=src)
-            elif op == "QV":
-                quant(v_codes[i][:], v_scales[i][:], v_bf[i][:].rearrange("p c e j -> p (c e j)"))
-            elif op == "SQ":
-                nc.scalar.activation(
-                    out=q_sq[i % 3][:].rearrange("p r m j -> p m j r")[:, :, :, sl],
-                    in_=q_raw[i][:].rearrange("p j (m r) -> p m j r", r=4)[:, :, :, sl],
-                    func=ACT.Square,
-                )
-            elif op == "VQ":
-                cols = slice(128 * sl.start, 128 * sl.stop)
-                nc.vector.scalar_tensor_tensor(
-                    out=fq[i][:, cols, :],
-                    in0=q_sq[i % 3][:].rearrange("p r m j -> p (r m) j")[:, cols, :],
-                    scalar=0.125,
-                    in1=qa_sb[:].unsqueeze(1).to_broadcast([P, 128 * n, 4]),
-                    op0=ALU.add,
-                    op1=ALU.mult,
-                )
-            elif op == "QQ":
-                cols = slice(128 * sl.start, 128 * sl.stop)
-                quant(q_codes[i][:, cols], q_scales[i][:, cols], fq[i][:, cols, :].rearrange("p n j -> p (n j)"))
-            elif op == "M1":
-                for x in range(4):
-                    for c in range(2):
-                        w = slice(768 * i + 192 * x + 64 * c, 768 * i + 192 * x + 64 * c + 128)
-                        e = slice(128 * c, 128 * c + 128)
-                        mm(state[i % 2][:, x, :], k_codes[:, w], k_scales[:, w], v_codes[i][:, e], v_scales[i][:, e], c == 0, c == 1)
-            elif op == "SC":
-                src = state[i % 2][:].rearrange("p x e -> p e x")
-                if name in ON_VECTOR:
-                    nc.vector.tensor_scalar(out=s_bf[i][:], in0=src, scalar1=1.0 / N, scalar2=None, op0=ALU.mult)
-                else:
-                    nc.scalar.activation(out=s_bf[i][:], in_=src, func=ACT.Copy, scale=1.0 / N)
-            elif op == "QS":
-                quant(s_codes[i][:], s_scales[i][:], s_bf[i][:].rearrange("p e x -> p (e x)"))
-            elif op == "M2":
-                for s in range(sl.start, sl.stop):
-                    for c in range(2):
-                        rows = slice(64 * c, 64 * c + 64)
-                        u = i
-                        m = slice(128 * s, 128 * s + 128)
-                        mm(bank(2 * i + c, part)[:, s, :], q_codes[u][rows, m], q_scales[u][rows, m], s_codes[i][rows, :], s_scales[i][rows, :], True, True)
-            elif op == "R":
-                r = rec[3 * i + {"": 0, "a": 0, "c": 1, "d": 2}[part]]
-                nc.vector.reciprocal(out=r[:, sl], in_=bank(i, part)[:, sl, E - 1])
-            elif op == "EV":
-                r = rec[3 * i + {"": 0, "a": 0, "c": 1, "d": 2}[part]]
-                dst = res[i // 2][:, i % 2]
-                if name in ON_VECTOR:
-                    nc.vector.tensor_tensor(
-                        out=dst[:, sl, :], in0=bank(i, part)[:, sl, :],
-                        in1=r[:, sl].unsqueeze(2).to_broadcast([P, n, E]), op=ALU.mult,
+        def cast_values(g, on_scalar=False):
+            dst = v_bf[g][:].rearrange("p c (f u) j -> p c f j u", u=4)
+            src = v_raw[g][:].rearrange("p c j (f u) -> p c f j u", u=4)
+            if on_scalar:
+                for c in range(2):
+                    nc.scalar.copy(out=dst[:, c], in_=src[:, c])
+            else:
+                nc.vector.tensor_copy(out=dst, in_=src)
+
+        def quantise_values(g):
+            quantise(v_codes[g][:], v_scales[g][:], v_bf[g][:].rearrange("p c e j -> p (c e j)"))
+
+        def build_state(g):
+            for x in range(PACK):
+                for c in range(2):
+                    word = PAIR_WORDS * g + GROUP * x + TILE * c
+                    words, cols = slice(word, word + P), slice(E * c, E * (c + 1))
+                    matmul(
+                        state[g % STATE_BANKS][:, x, :], k_codes[:, words], k_scales[:, words],
+                        v_codes[g][:, cols], v_scales[g][:, cols], c == 0, c == 1,
                     )
-                else:
-                    for s in range(sl.start, sl.stop):
-                        nc.scalar.activation(out=dst[:, s, :], in_=bank(i, part)[:, s, :], func=ACT.Copy, scale=r[:, s : s + 1])
-            elif op == "ST":
-                if part == "":
-                    nc.sync.dma_start(out=out[i].rearrange("(m r) e -> m r e", r=4), in_=res[i // 2][:, i % 2])
-                else:
-                    nc.sync.dma_start(
-                        out=out[2 * i : 2 * i + 2].rearrange("c (m r) e -> m c r e", r=4)[:, :, sl, :], in_=res[i][:, :, sl, :]
+
+        def round_state(g):
+            src = state[g % STATE_BANKS][:].rearrange("p x e -> p e x")
+            nc.scalar.activation(out=s_bf[g][:], in_=src, func=ACT.Copy, scale=1.0 / N)
+
+        def quantise_state(g):
+            quantise(s_codes[g][:], s_scales[g][:], s_bf[g][:].rearrange("p e x -> p (e x)"))
+
+        def square_queries(g, half=None):
+            square(q_sq[g % QUERY_SQUARE_BUFS][:], q_raw[g][:], half)
+
+        def map_queries(g, groups=ALL_GROUPS, half=None):
+            dst = q_bf[g][:].rearrange("p (r m) (hi lo) -> p r m hi lo", r=PACK, lo=2)[:, groups]
+            if half is not None:
+                dst = dst[:, :, P // 2 * half : P // 2 * (half + 1)]
+            sq = squares_by_word(q_sq[g % QUERY_SQUARE_BUFS][:], half)[:, groups]
+            factor = qa_sb[:].unsqueeze(1).to_broadcast([P, dst.shape[1] * dst.shape[2], PACK])
+            shift_and_weigh(dst, sq, factor)
+
+        def quantise_queries(g, groups=ALL_GROUPS):
+            cols = slice(P * groups.start, P * groups.stop)
+            quantise(q_codes[g][:, cols], q_scales[g][:, cols], q_bf[g][:, cols, :].rearrange("p n x -> p (n x)"))
+
+        def read_state(g, bank, groups=ALL_GROUPS):
+            for r in range(groups.start, groups.stop):
+                for c in range(2):
+                    rows, cols = slice(TILE * c, TILE * (c + 1)), slice(P * r, P * (r + 1))
+                    matmul(
+                        y_banks[c][bank][:, r, :], q_codes[g][rows, cols], q_scales[g][rows, cols],
+                        s_codes[g][rows, :], s_scales[g][rows, :], True, True,
                     )
+
+        def invert(h, bank, groups=ALL_GROUPS):
+            nc.vector.reciprocal(out=inv[h][:, groups], in_=y_banks[h % 2][bank][:, groups, E - 1])
+
+        def normalise(h, bank, groups=ALL_GROUPS, on_vector=False):
+            src, dst = y_banks[h % 2][bank], res[h // 2][:, h % 2]
+            if on_vector:
+                factor = inv[h][:, groups].unsqueeze(2).to_broadcast([P, groups.stop - groups.start, E])
+                nc.vector.tensor_tensor(out=dst[:, groups, :], in0=src[:, groups, :], in1=factor, op=ALU.mult)
+            else:
+                for r in range(groups.start, groups.stop):
+                    nc.scalar.activation(out=dst[:, r, :], in_=src[:, r, :], func=ACT.Copy, scale=inv[h][:, r : r + 1])
+
+        def finish_head(h):
+            normalise(h, h // 2)
+            nc.sync.dma_start(out=out[h].rearrange("(m r) e -> m r e", r=PACK), in_=res[h // 2][:, h % 2])
+
+        def store_part(g, groups):
+            rows = out[2 * g : 2 * g + 2].rearrange("c (m r) e -> m c r e", r=PACK)
+            nc.sync.dma_start(out=rows[:, :, groups, :], in_=res[g][:, :, groups, :])
 
         with tc.manual_schedule():
-            for name in LOADS:
-                load(name)
-            for name in ORDER:
-                run(name)
+            nc.sync.dma_start(out=ka_sb[:], in_=ka)
+            nc.sync.dma_start(out=t_sb[:], in_=t.rearrange("(p j) o -> p (j o)", j=PACK))
+            load_keys(0)
+            load_keys(1)
+            load_values(0)
+            load_keys(2)
+            load_keys(3)
+            load_queries(0)
+            for c in range(2):
+                nc.sync.dma_start(out=qa_sb[TILE * c : TILE * (c + 1), :], in_=qa.rearrange("(m x) o -> m (x o)", x=PACK))
+            load_queries(1)
+            load_values(1)
+            for g in (2, 3):
+                load_keys(2 * g)
+                load_keys(2 * g + 1)
+                load_values(g)
+            load_queries(2)
+            load_queries(3)
+
+            nc.vector.memset(k_codes[:].rearrange("p (b w) -> p b w", w=GROUP)[:, :, TILE : 2 * TILE], 0)
+            scale_words = k_scales[:].bitcast(U32).rearrange("p (b w) -> p b w", w=GROUP // 4)
+            nc.vector.memset(scale_words[:, :, TILE // 4 : 2 * TILE // 4], SCALE_BYTES_ONE)
+            nc.vector.tensor_tensor(
+                out=key_factor[:],
+                in0=ka_sb[:].rearrange("p (m x) -> p x m", x=PACK).unsqueeze(3).to_broadcast([P, PACK, TILE, PACK]),
+                in1=t_sb[:].unsqueeze(1).unsqueeze(1).to_broadcast([P, PACK, TILE, PACK]),
+                op=ALU.mult,
+            )
+
+            for h in (0, 1):
+                for half in (0, 1):
+                    square_keys(h, half)
+                    map_keys(h, half)
+            cast_values(0)
+            quantise_keys(0)
+            quantise_values(0)
+            build_state(0)
+            for h in (2, 3):
+                square_keys(h)
+                map_keys(h)
+            round_state(0)
+            quantise_state(0)
+            quantise_keys(1)
+
+            for half in (0, 1):
+                square_queries(0, half)
+                map_queries(0, half=half)
+            cast_values(1)
+            quantise_queries(0)
+            read_state(0, 0)
+            quantise_values(1)
+            build_state(1)
+            square_queries(1)
+            map_queries(1)
+            invert(0, 0)
+            invert(1, 0)
+
+            square_keys(4)
+            square_keys(5)
+            round_state(1)
+            map_keys(4)
+            quantise_state(1)
+            quantise_queries(1)
+            read_state(1, 1)
+            finish_head(0)
+            finish_head(1)
+            cast_values(2)
+            map_keys(5)
+            quantise_values(2)
+            quantise_keys(2)
+            build_state(2)
+            invert(2, 1)
+            invert(3, 1)
+            for h in (6, 7):
+                square_keys(h)
+                map_keys(h)
+            cast_values(3, on_scalar=True)
+            quantise_values(3)
+            quantise_keys(3)
+            build_state(3)
+
+            square_queries(2)
+            round_state(2)
+            map_queries(2)
+            quantise_state(2)
+            quantise_queries(2)
+            read_state(2, 2)
+            square_queries(3)
+            round_state(3)
+            first, second, third = LAST_PARTS
+            map_queries(3, first)
+            quantise_state(3)
+            invert(4, 2)
+            quantise_queries(3, first)
+            read_state(3, 0, first)
+            invert(5, 2)
+            for h in (2, 3, 4, 5):
+                finish_head(h)
+
+            map_queries(3, second)
+            map_queries(3, third)
+            invert(6, 0, first)
+            invert(7, 0, first)
+            quantise_queries(3, second)
+            read_state(3, 1, second)
+            normalise(6, 0, first, on_vector=True)
+            normalise(7, 0, first)
+            store_part(3, first)
+            quantise_queries(3, third)
+            read_state(3, 2, third)
+            for h in (6, 7):
+                invert(h, 1, second)
+            for h in (6, 7):
+                normalise(h, 1, second)
+            store_part(3, second)
+            for h in (6, 7):
+                invert(h, 2, third)
+            normalise(6, 2, third)
+            normalise(7, 2, third, on_vector=True)
+            store_part(3, third)

from contextlib import ExitStack

import concourse.mybir as mybir

H, D, N, E = 8, 256, 512, 128
FLOPS = 2 * (2 * H * N * D * E)

F32 = mybir.dt.float32
BF16 = mybir.dt.bfloat16
U32 = mybir.dt.uint32
U8 = mybir.dt.uint8
FP8X4 = mybir.dt.float8_e4m3fn_x4
ACT = mybir.ActivationFunctionType
ALU = mybir.AluOpType

P = 128
PACK = 4
TILE = D // PACK
PAIRS = H // 2
GROUP = 3 * TILE
PAIR_WORDS = PACK * GROUP
PHI_SHIFT = 0.125
SCALE_BYTES_ONE = 0x01010101

KEY_SQUARE_BUFS = 6
QUERY_SQUARE_BUFS = 3
STATE_BANKS = 2
ROW_TILE_BANKS = 3

ALL_GROUPS = slice(0, PACK)
LAST_PARTS = (slice(0, 2), slice(2, 3), slice(3, 4))


def tile_rows_lin_sq_norm_kernel(tc, q, qa, ka, k, t, v, out):
    nc = tc.nc
    with ExitStack() as ctx:
        sb = ctx.enter_context(tc.tile_pool(name="sb", bufs=1))
        ps = ctx.enter_context(tc.psum_pool(name="ps", bufs=1))

        def tiles(name, count, shape, dtype):
            return [sb.tile(shape, dtype, name="%s%d" % (name, i), align_bytes=64) for i in range(count)]

        t_sb = sb.tile([P, PACK], F32, name="t_sb")
        qa_sb = sb.tile([P, PACK], F32, name="qa_sb")
        ka_sb = sb.tile([P, D], F32, name="ka_sb")
        key_factor = sb.tile([P, PACK, TILE, PACK], F32, name="key_factor", align_bytes=64)
        k_raw = tiles("k_raw", H, [P, PACK, D], F32)
        k_sq = tiles("k_sq", KEY_SQUARE_BUFS, [P, 2, 2 * D], F32)
        k_bf = tiles("k_bf", PAIRS, [P, PACK, 2, TILE * PACK], BF16)
        k_codes = sb.tile([P, PAIRS * PAIR_WORDS], U32, name="k_codes", align_bytes=64)
        k_scales = sb.tile([P, PAIRS * PAIR_WORDS], U8, name="k_scales", align_bytes=64)
        v_raw = tiles("v_raw", PAIRS, [P, 2, PACK, E], F32)
        v_bf = tiles("v_bf", PAIRS, [P, 2, E, PACK], BF16)
        v_codes = tiles("v_codes", PAIRS, [P, 2 * E], U32)
        v_scales = tiles("v_scales", PAIRS, [P, 2 * E], U8)
        q_raw = tiles("q_raw", PAIRS, [P, PACK, N], F32)
        q_sq = tiles("q_sq", QUERY_SQUARE_BUFS, [P, 2, 2 * N], F32)
        q_bf = tiles("q_bf", PAIRS, [P, N, PACK], BF16)
        q_codes = tiles("q_codes", PAIRS, [P, N], U32)
        q_scales = tiles("q_scales", PAIRS, [P, N], U8)
        s_bf = tiles("s_bf", PAIRS, [P, E, PACK], BF16)
        s_codes = tiles("s_codes", PAIRS, [P, E], U32)
        s_scales = tiles("s_scales", PAIRS, [P, E], U8)
        inv = tiles("inv", H, [P, PACK], F32)
        res = tiles("res", PAIRS, [P, 2, PACK, E], F32)
        state = [ps.tile([P, PACK, E], F32, name="state%d" % i) for i in range(STATE_BANKS)]
        y_banks = [[ps.tile([P, PACK, E], F32, name="y%d_%d" % (c, i)) for i in range(ROW_TILE_BANKS)] for c in range(2)]

        def load_keys(h):
            nc.sync.dma_start(out=k_raw[h][:], in_=k[h].rearrange("(p j) d -> p j d", j=PACK))

        def load_values(g):
            nc.sync.dma_start(out=v_raw[g][:], in_=v[2 * g : 2 * g + 2].rearrange("c (p j) e -> p c j e", j=PACK))

        def load_queries(g):
            nc.sync.dma_start(out=q_raw[g][:], in_=q[2 * g : 2 * g + 2].rearrange("c (m x) n -> (c m) x n", x=PACK))

        def quantise(codes, scales, src):
            nc.vector.quantize_mx(out=codes.bitcast(FP8X4), scales=scales, in_=src)

        def matmul(dst, lhs_codes, lhs_scales, rhs_codes, rhs_scales, start, stop):
            nc.tensor.matmul_mx(
                out=dst,
                lhsT=lhs_codes.bitcast(FP8X4),
                lhsT_scale=lhs_scales,
                rhs=rhs_codes.bitcast(FP8X4),
                rhs_scale=rhs_scales,
                start=start,
                stop=stop,
            )

        def square(dst, raw, half):
            rows = raw.rearrange("p (hi lo) (m g) -> p lo m g hi", lo=2, g=PACK)
            if half is None:
                cols = dst.rearrange("p lo (g m hi) -> p lo m g hi", g=PACK, hi=2)
            else:
                cols = dst.rearrange("p lo (a g m hi) -> p a lo m g hi", a=2, g=PACK, hi=2)[:, half]
                width = cols.shape[2]
                rows = rows[:, :, width * half : width * (half + 1)]
            for lo in range(2):
                nc.scalar.activation(out=cols[:, lo], in_=rows[:, lo], func=ACT.Square)

        def squares_by_word(sq, half):
            if half is None:
                return sq.rearrange("p lo (g m hi) -> p g m hi lo", g=PACK, hi=2)
            return sq.rearrange("p lo (a g m hi) -> p a g m hi lo", a=2, g=PACK, hi=2)[:, half]

        def shift_and_weigh(dst, sq, factor):
            nc.vector.scalar_tensor_tensor(out=dst, in0=sq, scalar=PHI_SHIFT, in1=factor, op0=ALU.add, op1=ALU.mult)

        def square_keys(h, half=None):
            square(k_sq[h % KEY_SQUARE_BUFS][:], k_raw[h][:], half)

        def map_keys(h, half=None):
            g, c = divmod(h, 2)
            dst = k_bf[g][:, :, c, :].rearrange("p x (m hi lo) -> p x m hi lo", hi=2, lo=2)
            factor = key_factor[:].rearrange("p x m (hi lo) -> p x m hi lo", lo=2)
            if half is not None:
                cols = slice(TILE // 2 * half, TILE // 2 * (half + 1))
                dst, factor = dst[:, :, cols], factor[:, :, cols]
            shift_and_weigh(dst, squares_by_word(k_sq[h % KEY_SQUARE_BUFS][:], half), factor)

        def quantise_keys(g):
            flat = k_bf[g][:].rearrange("p x c w -> p (x c w)")
            heads = [(0, 1)] + [(2 * x + 1, 2) for x in range(PACK - 1)] + [(2 * PACK - 1, 1)]
            for first, count in heads:
                word = PAIR_WORDS * g + GROUP * (first // 2) + 2 * TILE * (first % 2)
                words = slice(word, word + TILE * count)
                quantise(k_codes[:, words], k_scales[:, words], flat[:, D * first : D * (first + count)])

        def cast_values(g, on_scalar=False):
            dst = v_bf[g][:].rearrange("p c (f u) j -> p c f j u", u=4)
            src = v_raw[g][:].rearrange("p c j (f u) -> p c f j u", u=4)
            if on_scalar:
                for c in range(2):
                    nc.scalar.copy(out=dst[:, c], in_=src[:, c])
            else:
                nc.vector.tensor_copy(out=dst, in_=src)

        def quantise_values(g):
            quantise(v_codes[g][:], v_scales[g][:], v_bf[g][:].rearrange("p c e j -> p (c e j)"))

        def build_state(g):
            for x in range(PACK):
                for c in range(2):
                    word = PAIR_WORDS * g + GROUP * x + TILE * c
                    words, cols = slice(word, word + P), slice(E * c, E * (c + 1))
                    matmul(
                        state[g % STATE_BANKS][:, x, :], k_codes[:, words], k_scales[:, words],
                        v_codes[g][:, cols], v_scales[g][:, cols], c == 0, c == 1,
                    )

        def round_state(g):
            src = state[g % STATE_BANKS][:].rearrange("p x e -> p e x")
            nc.scalar.activation(out=s_bf[g][:], in_=src, func=ACT.Copy, scale=1.0 / N)

        def quantise_state(g):
            quantise(s_codes[g][:], s_scales[g][:], s_bf[g][:].rearrange("p e x -> p (e x)"))

        def square_queries(g, half=None):
            square(q_sq[g % QUERY_SQUARE_BUFS][:], q_raw[g][:], half)

        def map_queries(g, groups=ALL_GROUPS, half=None):
            dst = q_bf[g][:].rearrange("p (r m) (hi lo) -> p r m hi lo", r=PACK, lo=2)[:, groups]
            if half is not None:
                dst = dst[:, :, P // 2 * half : P // 2 * (half + 1)]
            sq = squares_by_word(q_sq[g % QUERY_SQUARE_BUFS][:], half)[:, groups]
            factor = qa_sb[:].unsqueeze(1).to_broadcast([P, dst.shape[1] * dst.shape[2], PACK])
            shift_and_weigh(dst, sq, factor)

        def quantise_queries(g, groups=ALL_GROUPS):
            cols = slice(P * groups.start, P * groups.stop)
            quantise(q_codes[g][:, cols], q_scales[g][:, cols], q_bf[g][:, cols, :].rearrange("p n x -> p (n x)"))

        def read_state(g, bank, groups=ALL_GROUPS):
            for r in range(groups.start, groups.stop):
                for c in range(2):
                    rows, cols = slice(TILE * c, TILE * (c + 1)), slice(P * r, P * (r + 1))
                    matmul(
                        y_banks[c][bank][:, r, :], q_codes[g][rows, cols], q_scales[g][rows, cols],
                        s_codes[g][rows, :], s_scales[g][rows, :], True, True,
                    )

        def invert(h, bank, groups=ALL_GROUPS):
            nc.vector.reciprocal(out=inv[h][:, groups], in_=y_banks[h % 2][bank][:, groups, E - 1])

        def normalise(h, bank, groups=ALL_GROUPS, on_vector=False):
            src, dst = y_banks[h % 2][bank], res[h // 2][:, h % 2]
            if on_vector:
                factor = inv[h][:, groups].unsqueeze(2).to_broadcast([P, groups.stop - groups.start, E])
                nc.vector.tensor_tensor(out=dst[:, groups, :], in0=src[:, groups, :], in1=factor, op=ALU.mult)
            else:
                for r in range(groups.start, groups.stop):
                    nc.scalar.activation(out=dst[:, r, :], in_=src[:, r, :], func=ACT.Copy, scale=inv[h][:, r : r + 1])

        def finish_head(h):
            normalise(h, h // 2)
            nc.sync.dma_start(out=out[h].rearrange("(m r) e -> m r e", r=PACK), in_=res[h // 2][:, h % 2])

        def store_part(g, groups):
            rows = out[2 * g : 2 * g + 2].rearrange("c (m r) e -> m c r e", r=PACK)
            nc.sync.dma_start(out=rows[:, :, groups, :], in_=res[g][:, :, groups, :])

        with tc.manual_schedule():
            nc.sync.dma_start(out=ka_sb[:], in_=ka)
            nc.sync.dma_start(out=t_sb[:], in_=t.rearrange("(p j) o -> p (j o)", j=PACK))
            load_keys(0)
            load_keys(1)
            load_values(0)
            load_keys(2)
            load_keys(3)
            load_queries(0)
            for c in range(2):
                nc.sync.dma_start(out=qa_sb[TILE * c : TILE * (c + 1), :], in_=qa.rearrange("(m x) o -> m (x o)", x=PACK))
            load_queries(1)
            load_values(1)
            for g in (2, 3):
                load_keys(2 * g)
                load_keys(2 * g + 1)
                load_values(g)
            load_queries(2)
            load_queries(3)

            nc.vector.memset(k_codes[:].rearrange("p (b w) -> p b w", w=GROUP)[:, :, TILE : 2 * TILE], 0)
            scale_words = k_scales[:].bitcast(U32).rearrange("p (b w) -> p b w", w=GROUP // 4)
            nc.vector.memset(scale_words[:, :, TILE // 4 : 2 * TILE // 4], SCALE_BYTES_ONE)
            nc.vector.tensor_tensor(
                out=key_factor[:],
                in0=ka_sb[:].rearrange("p (m x) -> p x m", x=PACK).unsqueeze(3).to_broadcast([P, PACK, TILE, PACK]),
                in1=t_sb[:].unsqueeze(1).unsqueeze(1).to_broadcast([P, PACK, TILE, PACK]),
                op=ALU.mult,
            )

            for h in (0, 1):
                for half in (0, 1):
                    square_keys(h, half)
                    map_keys(h, half)
            cast_values(0)
            quantise_keys(0)
            quantise_values(0)
            build_state(0)
            for h in (2, 3):
                square_keys(h)
                map_keys(h)
            round_state(0)
            quantise_state(0)
            quantise_keys(1)

            for half in (0, 1):
                square_queries(0, half)
                map_queries(0, half=half)
            cast_values(1)
            quantise_queries(0)
            read_state(0, 0)
            quantise_values(1)
            build_state(1)
            square_queries(1)
            map_queries(1)
            invert(0, 0)
            invert(1, 0)

            square_keys(4)
            square_keys(5)
            round_state(1)
            map_keys(4)
            quantise_state(1)
            quantise_queries(1)
            read_state(1, 1)
            finish_head(0)
            finish_head(1)
            cast_values(2)
            map_keys(5)
            quantise_values(2)
            quantise_keys(2)
            build_state(2)
            invert(2, 1)
            invert(3, 1)
            for h in (6, 7):
                square_keys(h)
                map_keys(h)
            cast_values(3, on_scalar=True)
            quantise_values(3)
            quantise_keys(3)
            build_state(3)

            square_queries(2)
            round_state(2)
            map_queries(2)
            quantise_state(2)
            quantise_queries(2)
            read_state(2, 2)
            square_queries(3)
            round_state(3)
            first, second, third = LAST_PARTS
            map_queries(3, first)
            quantise_state(3)
            invert(4, 2)
            quantise_queries(3, first)
            read_state(3, 0, first)
            invert(5, 2)
            for h in (2, 3, 4, 5):
                finish_head(h)

            map_queries(3, second)
            map_queries(3, third)
            invert(6, 0, first)
            invert(7, 0, first)
            quantise_queries(3, second)
            read_state(3, 1, second)
            normalise(6, 0, first, on_vector=True)
            normalise(7, 0, first)
            store_part(3, first)
            quantise_queries(3, third)
            read_state(3, 2, third)
            for h in (6, 7):
                invert(h, 1, second)
            for h in (6, 7):
                normalise(h, 1, second)
            store_part(3, second)
            for h in (6, 7):
                invert(h, 2, third)
            normalise(6, 2, third)
            normalise(7, 2, third, on_vector=True)
            store_part(3, third)
